import numpy as np
import ml_dtypes


def mxq(x, axis, fmt="e4m3"):
    dtype, down = {"e4m3": (ml_dtypes.float8_e4m3fn, 7), "e5m2": (ml_dtypes.float8_e5m2, 14)}[fmt]
    v = np.moveaxis(np.asarray(x, np.float32).astype(ml_dtypes.bfloat16).astype(np.float64), axis, -1)
    blocks = v.reshape(v.shape[:-1] + (-1, 32))
    amax = np.abs(blocks).max(-1, keepdims=True)
    byte = np.maximum(np.where(amax > 0, np.frexp(amax)[1] - 1 + 127, 0) - down, 1)
    scale = np.exp2(byte - 127.0)
    codes = (blocks / scale).astype(np.float32).astype(dtype).astype(np.float64)
    return np.moveaxis((codes * scale).reshape(v.shape), -1, axis)


WIDE = False


def mx_kscale(k):
    if not WIDE:
        return np.ones(k)
    levels = np.array([10, -10, 5, -5, 0])
    if k % 512:
        return np.exp2(np.random.permutation(np.resize(levels, k // 32))).repeat(32)
    a = np.empty((k // 512, 16))
    for p in range(k // 512):
        a[p, :8] = np.random.permutation(np.resize(levels, 8))
        for g in range(8):
            far = levels[np.abs(levels - a[p, g]) >= 10]
            a[p, g + 8] = far[np.random.randint(len(far))]
    return np.exp2(a.ravel()).repeat(32)


def f64(x):
    return np.asarray(x).astype(np.float64)


def striped8(idx):
    return np.asarray(idx).reshape(8, -1, 16).transpose(0, 2, 1).reshape(128, -1).astype(np.uint16)


def unstriped8(offs):
    return offs.reshape(8, 16, -1).transpose(0, 2, 1).reshape(8, -1).astype(np.int64)


def pick8(x, idx, run):
    r = np.arange(len(x))
    return x[r[:, None], idx[r % (8 * run) // run]]


E2M1 = np.array([0.0, 0.5, 1.0, 1.5, 2.0, 3.0, 4.0, 6.0, -0.0, -0.5, -1.0, -1.5, -2.0, -3.0, -4.0, -6.0])


def pack_weight(w, fmt):
    k, n = w.shape
    w = f64(np.asarray(w, np.float32).astype(ml_dtypes.bfloat16)).reshape(k // 32, 32, n)
    amax = np.abs(w).max(1)
    if fmt == "e4m3":
        byte = np.frexp(amax)[1] - 1 + 127 - 7
    else:
        mant, ex = np.frexp(amax / 6.0)
        byte = np.where(mant > 0.5, ex, ex - 1) + 127
    byte = np.clip(np.where(amax > 0, byte, 1), 1, 254)
    scaled = (w * np.exp2(127.0 - byte)[:, None, :]).reshape(k, n).astype(np.float32)
    by_word = np.ascontiguousarray(scaled.reshape(k // 512, 128, 4, n).transpose(0, 1, 3, 2))
    if fmt == "e4m3":
        words = by_word.astype(ml_dtypes.float8_e4m3fn).view(np.uint8)
    else:
        c = by_word.astype(ml_dtypes.float4_e2m1fn).view(np.uint8) & 0xF
        words = (c[..., 0::2] | (c[..., 1::2] << 4)).reshape(k // 512, 128, 2 * n)
    return np.ascontiguousarray(words), np.ascontiguousarray(byte.astype(np.uint8).reshape(k // 512, 16, n))


def unpack_weight(words, scales, fmt):
    g, _, n = scales.shape
    words = np.ascontiguousarray(words).reshape(g, 128, n, -1)
    if fmt == "e4m3":
        vals = words.view(ml_dtypes.float8_e4m3fn).astype(np.float64)
    else:
        nib = np.empty((g, 128, n, 4), np.uint8)
        nib[..., 0::2] = words & 0xF
        nib[..., 1::2] = words >> 4
        vals = E2M1[nib]
    vals = vals * np.repeat(np.exp2(scales.astype(np.float64) - 127.0), 8, axis=1)[..., None]
    return vals.transpose(0, 1, 3, 2).reshape(g * 512, n)


D, T, I, Q = 512, 1024, 512, 128


def setup_inputs():
    n = np.random.standard_normal
    idx = np.stack([np.random.permutation(T)[:I] for _ in range(8)])
    idx2 = np.stack([np.random.permutation(T)[:I] for _ in range(8)])
    idx3 = np.stack([np.random.permutation(T)[:I] for _ in range(8)])
    idx4 = np.stack([np.random.permutation(T)[:I] for _ in range(8)])
    fd = mx_kscale(D)
    keysp = pack_weight(n((D, T)) / fd[:, None], "e4m3")
    return {
        "query": (n((D, Q)) * 0.9 / np.sqrt(D) * fd[:, None]).astype(np.float32),
        "query2": (n((D, Q)) * 0.9 / np.sqrt(D) * fd[:, None]).astype(np.float32),
        "keys_words": keysp[0],
        "keys_scales": keysp[1],
        "lam": (np.random.uniform(0.5, 1.3, (Q, 1))).astype(np.float32),
        "old": (1.0 * n((Q, T))).astype(np.float32),
        "offs": striped8(idx),
        "offs2": striped8(idx2),
        "offs3": striped8(idx3),
        "offs4": striped8(idx4),
    }


def reference(query, query2, keys_words, keys_scales, lam, old, offs, offs2, offs3, offs4):
    idx = unstriped8(offs)
    idx2 = unstriped8(offs2)
    idx3 = unstriped8(offs3)
    idx4 = unstriped8(offs4)
    keysu = unpack_weight(keys_words, keys_scales, "e4m3")
    queryq = mxq(f64(query), 0, "e4m3")
    a = queryq.T @ keysu
    query2q = mxq(f64(query2), 0, "e4m3")
    b = query2q.T @ keysu
    w = (np.maximum(pick8(a, idx, 16), pick8(b, idx2, 16)) - np.maximum(pick8(a, idx2, 16), pick8(b, idx, 16))) * f64(lam)
    f1 = np.zeros((Q, T))
    f1[np.arange(Q)[:, None], idx[np.arange(Q) % 128 // 16]] = w
    f2 = f1 + f64(old)
    y = np.maximum(pick8(f2, idx3, 16), pick8(f2, idx4, 16))
    return y

@@ -1,0 +1,155 @@
+from contextlib import ExitStack
+
+import concourse.mybir as mybir
+
+D, T, I, Q = 512, 1024, 512, 128
+FLOPS = 2 * 2 * D * T * Q
+
+F32 = mybir.dt.float32
+BF16 = mybir.dt.bfloat16
+I32 = mybir.dt.int32
+U32 = mybir.dt.uint32
+U16 = mybir.dt.uint16
+U8 = mybir.dt.uint8
+FP8X4 = mybir.dt.float8_e4m3fn_x4
+ALU = mybir.AluOpType
+COPY = mybir.ActivationFunctionType.Copy
+
+P = 128
+PACK = 4
+CHUNK = 256
+HALF = I // 2
+PIECE = HALF // 2
+STRIPE = 16
+
+
+def tile_attend_exchanged_lean_throughtwo_heads_kernel(
+    tc, query, query2, keys_words, keys_scales, lam, old, offs, offs2, offs3, offs4, out
+):
+    nc = tc.nc
+    with ExitStack() as ctx:
+        sb = ctx.enter_context(tc.tile_pool(name="sb", bufs=1))
+        ps = ctx.enter_context(tc.psum_pool(name="ps", bufs=1))
+
+        def entries(lst, start, count):
+            return lst[:, start // STRIPE : (start + count) // STRIPE]
+
+        key_scales = sb.tile([P, T], U8, align_bytes=64, name="key_scales")
+        nc.vector.memset(key_scales[:].bitcast(I32), 0)
+        for quad in range(4):
+            nc.scalar.dma_start(
+                out=key_scales[32 * quad : 32 * quad + 4, :].bitcast(I32),
+                in_=keys_scales[0, 4 * quad : 4 * quad + 4, :].bitcast(I32),
+            )
+
+        words_hbm = keys_words[0].rearrange("p n t -> p (n t)").bitcast(I32)
+        raw = []
+        key_words = []
+        for h, src in enumerate((query, query2)):
+            r = sb.tile([P, PACK, Q], F32, name="raw%d" % h)
+            nc.sync.dma_start(out=r[:], in_=src.rearrange("(p j) q -> p j q", j=PACK))
+            raw.append(r)
+            kw = sb.tile([P, T // 2], I32, align_bytes=64, name="key_words%d" % h)
+            nc.sync.dma_start(out=kw[:], in_=words_hbm[:, h * (T // 2) : (h + 1) * (T // 2)])
+            key_words.append(kw)
+
+        list1 = sb.tile([P, I // STRIPE], U16, name="list1")
+        nc.sync.dma_start(list1[:], offs)
+        list2 = sb.tile([P, I // STRIPE], U16, name="list2")
+        nc.sync.dma_start(list2[:], offs2)
+        lam_col = sb.tile([P, 1], F32, name="lam_col")
+        nc.gpsimd.dma_start(out=lam_col[:], in_=lam)
+        old_sb = sb.tile([P, T], F32, name="old_sb")
+        nc.sync.dma_start(out=old_sb[:], in_=old)
+        list3 = sb.tile([P, I // STRIPE], U16, name="list3")
+        nc.sync.dma_start(list3[:], offs3)
+        list4 = sb.tile([P, I // STRIPE], U16, name="list4")
+        nc.sync.dma_start(list4[:], offs4)
+
+        f1 = sb.tile([P, T], F32, name="f1")
+        nc.vector.memset(f1[:], 0.0)
+        lam_wide = sb.tile([P, PIECE], F32, name="lam_wide")
+        nc.scalar.copy(out=lam_wide[:], in_=lam_col[:].to_broadcast([P, PIECE]))
+
+        codes = []
+        for h in range(2):
+            grouped = sb.tile([P, Q, PACK], BF16, align_bytes=64, name="grouped%d" % h)
+            nc.vector.tensor_copy(
+                out=grouped[:].rearrange("p (c i) t -> p c t i", i=4),
+                in_=raw[h][:].rearrange("p t (c i) -> p c t i", i=4),
+            )
+            qc = sb.tile([P, Q], U32, align_bytes=64, name="q_codes%d" % h)
+            qs = sb.tile([P, Q], U8, align_bytes=64, name="q_scales%d" % h)
+            nc.vector.quantize_mx(
+                out=qc[:].bitcast(FP8X4), scales=qs[:], in_=grouped[:].rearrange("p q t -> p (q t)")
+            )
+            codes.append((qc, qs))
+
+        def scores(h, name, on_vector):
+            table = sb.tile([P, T], F32, name=name)
+            qc, qs = codes[h]
+            for c in range(T // CHUNK):
+                bank = ps.tile([P, CHUNK], F32, name="bank_%s%d" % (name, c))
+                kw = key_words[c * CHUNK // (T // 2)]
+                k0 = c * CHUNK % (T // 2)
+                nc.tensor.matmul_mx(
+                    out=bank[:],
+                    lhsT=qc[:].bitcast(FP8X4),
+                    lhsT_scale=qs[:],
+                    rhs=kw[:, k0 : k0 + CHUNK].bitcast(FP8X4),
+                    rhs_scale=key_scales[:, c * CHUNK : (c + 1) * CHUNK],
+                    start=True,
+                    stop=True,
+                )
+                cols = table[:, c * CHUNK : (c + 1) * CHUNK]
+                if c in on_vector:
+                    nc.vector.tensor_copy(out=cols, in_=bank[:])
+                else:
+                    nc.scalar.copy(out=cols, in_=bank[:])
+            return table
+
+        def look_up(on_vector, table, lst, half, name):
+            got = sb.tile([P, HALF], F32, name=name)
+            window = table[:].indirect(entries(lst, half * HALF, HALF))
+            if on_vector:
+                nc.vector.tensor_copy(got[:], window)
+            else:
+                nc.scalar.activation(got[:], window, COPY)
+            return got
+
+        a = scores(0, "a", (3,))
+        b = scores(1, "b", ())
+
+        picked = []
+        for half in range(2):
+            first = half == 0
+            a1 = look_up(first, a, list1, half, "a1_%d" % half)
+            a2 = look_up(first, a, list2, half, "a2_%d" % half)
+            b1 = look_up(False, b, list1, half, "b1_%d" % half)
+            b2 = look_up(first, b, list2, half, "b2_%d" % half)
+            picked.append((a1, a2, b1, b2))
+
+        for half in range(2):
+            a1, a2, b1, b2 = picked[half]
+            pieces = [slice(k * PIECE, (k + 1) * PIECE) for k in range(2)]
+            kept = [sb.tile([P, PIECE], F32, name="kept%d_%d" % (half, k)) for k in range(2)]
+            swapped = [sb.tile([P, PIECE], F32, name="swapped%d_%d" % (half, k)) for k in range(2)]
+            diff = [sb.tile([P, PIECE], F32, name="diff%d_%d" % (half, k)) for k in range(2)]
+            for k in range(2):
+                nc.vector.tensor_tensor(swapped[k][:], a2[:, pieces[k]], b1[:, pieces[k]], ALU.max)
+                nc.vector.tensor_tensor(kept[k][:], a1[:, pieces[k]], b2[:, pieces[k]], ALU.max)
+            for k in range(2):
+                nc.vector.tensor_tensor(diff[k][:], kept[k][:], swapped[k][:], ALU.subtract)
+            for k in range(2):
+                places = f1[:].indirect(entries(list1, half * HALF + k * PIECE, PIECE))
+                nc.vector.tensor_tensor(places, diff[k][:], lam_wide[:], ALU.mult)
+
+        f2 = sb.tile([P, T], F32, name="f2")
+        nc.vector.tensor_tensor(f2[:], f1[:], old_sb[:], ALU.add)
+
+        for half in range(2):
+            y4 = look_up(False, f2, list4, half, "y4_%d" % half)
+            y3 = look_up(True, f2, list3, half, "y3_%d" % half)
+            y = sb.tile([P, HALF], F32, name="y%d" % half)
+            nc.vector.tensor_tensor(y[:], y3[:], y4[:], ALU.max)
+            nc.sync.dma_start(out=out[:, half * HALF : (half + 1) * HALF], in_=y[:])

@@ -21,6 +21,7 @@ CHUNK = 256
 HALF = I // 2
 PIECE = HALF // 2
 STRIPE = 16
+KEY_LOADS = ((0, 3 * CHUNK), (3 * CHUNK, T))
 
 
 def tile_attend_exchanged_lean_throughtwo_heads_kernel(
@@ -34,13 +35,9 @@ def tile_attend_exchanged_lean_throughtwo_heads_kernel(
         def entries(lst, start, count):
             return lst[:, start // STRIPE : (start + count) // STRIPE]
 
-        key_scales = sb.tile([P, T], U8, align_bytes=64, name="key_scales")
-        nc.vector.memset(key_scales[:].bitcast(I32), 0)
-        for quad in range(4):
-            nc.scalar.dma_start(
-                out=key_scales[32 * quad : 32 * quad + 4, :].bitcast(I32),
-                in_=keys_scales[0, 4 * quad : 4 * quad + 4, :].bitcast(I32),
-            )
+        key_scales = sb.tile([P, CHUNK], U8, align_bytes=64, name="key_scales")
+        nc.gpsimd.memset(key_scales[:].bitcast(I32), 0)
+        scale_rows = keys_scales[0].bitcast(I32)
 
         words_hbm = keys_words[0].rearrange("p n t -> p (n t)").bitcast(I32)
         raw = []
@@ -49,8 +46,15 @@ def tile_attend_exchanged_lean_throughtwo_heads_kernel(
             r = sb.tile([P, PACK, Q], F32, name="raw%d" % h)
             nc.sync.dma_start(out=r[:], in_=src.rearrange("(p j) q -> p j q", j=PACK))
             raw.append(r)
-            kw = sb.tile([P, T // 2], I32, align_bytes=64, name="key_words%d" % h)
-            nc.sync.dma_start(out=kw[:], in_=words_hbm[:, h * (T // 2) : (h + 1) * (T // 2)])
+            if h == 0:
+                for quad in range(4):
+                    nc.sync.dma_start(
+                        out=key_scales[32 * quad : 32 * quad + 16, :].bitcast(I32),
+                        in_=scale_rows[4 * quad : 4 * quad + 4, :].rearrange("r (c n) -> c r n", c=4),
+                    )
+            lo, hi = KEY_LOADS[h]
+            kw = sb.tile([P, hi - lo], I32, align_bytes=64, name="key_words%d" % h)
+            nc.sync.dma_start(out=kw[:], in_=words_hbm[:, lo:hi])
             key_words.append(kw)
 
         list1 = sb.tile([P, I // STRIPE], U16, name="list1")
@@ -58,7 +62,7 @@ def tile_attend_exchanged_lean_throughtwo_heads_kernel(
         list2 = sb.tile([P, I // STRIPE], U16, name="list2")
         nc.sync.dma_start(list2[:], offs2)
         lam_col = sb.tile([P, 1], F32, name="lam_col")
-        nc.gpsimd.dma_start(out=lam_col[:], in_=lam)
+        nc.sync.dma_start(out=lam_col[:], in_=lam)
         old_sb = sb.tile([P, T], F32, name="old_sb")
         nc.sync.dma_start(out=old_sb[:], in_=old)
         list3 = sb.tile([P, I // STRIPE], U16, name="list3")
@@ -69,15 +73,17 @@ def tile_attend_exchanged_lean_throughtwo_heads_kernel(
         f1 = sb.tile([P, T], F32, name="f1")
         nc.vector.memset(f1[:], 0.0)
         lam_wide = sb.tile([P, PIECE], F32, name="lam_wide")
-        nc.scalar.copy(out=lam_wide[:], in_=lam_col[:].to_broadcast([P, PIECE]))
+        nc.gpsimd.tensor_scalar(lam_wide[:], lam_col[:].to_broadcast([P, PIECE]), 1.0, 0.0, ALU.mult, ALU.add)
 
         codes = []
         for h in range(2):
             grouped = sb.tile([P, Q, PACK], BF16, align_bytes=64, name="grouped%d" % h)
-            nc.vector.tensor_copy(
-                out=grouped[:].rearrange("p (c i) t -> p c t i", i=4),
-                in_=raw[h][:].rearrange("p t (c i) -> p c t i", i=4),
-            )
+            shares = ((nc.vector.tensor_copy, 0, Q // 2), (nc.scalar.copy, Q // 2, Q)) if h == 0 else ((nc.vector.tensor_copy, 0, Q),)
+            for copy, lo, hi in shares:
+                copy(
+                    out=grouped[:, lo:hi, :].rearrange("p (c i) t -> p c t i", i=4),
+                    in_=raw[h][:, :, lo:hi].rearrange("p t (c i) -> p c t i", i=4),
+                )
             qc = sb.tile([P, Q], U32, align_bytes=64, name="q_codes%d" % h)
             qs = sb.tile([P, Q], U8, align_bytes=64, name="q_scales%d" % h)
             nc.vector.quantize_mx(
@@ -90,14 +96,15 @@ def tile_attend_exchanged_lean_throughtwo_heads_kernel(
             qc, qs = codes[h]
             for c in range(T // CHUNK):
                 bank = ps.tile([P, CHUNK], F32, name="bank_%s%d" % (name, c))
-                kw = key_words[c * CHUNK // (T // 2)]
-                k0 = c * CHUNK % (T // 2)
+                part = c * CHUNK // KEY_LOADS[1][0]
+                kw = key_words[part]
+                k0 = c * CHUNK - KEY_LOADS[part][0]
                 nc.tensor.matmul_mx(
                     out=bank[:],
                     lhsT=qc[:].bitcast(FP8X4),
                     lhsT_scale=qs[:],
                     rhs=kw[:, k0 : k0 + CHUNK].bitcast(FP8X4),
-                    rhs_scale=key_scales[:, c * CHUNK : (c + 1) * CHUNK],
+                    rhs_scale=key_scales[4 * c : P, :],
                     start=True,
                     stop=True,
                 )
@@ -120,17 +127,12 @@ def tile_attend_exchanged_lean_throughtwo_heads_kernel(
         a = scores(0, "a", (3,))
         b = scores(1, "b", ())
 
-        picked = []
         for half in range(2):
             first = half == 0
-            a1 = look_up(first, a, list1, half, "a1_%d" % half)
-            a2 = look_up(first, a, list2, half, "a2_%d" % half)
             b1 = look_up(False, b, list1, half, "b1_%d" % half)
             b2 = look_up(first, b, list2, half, "b2_%d" % half)
-            picked.append((a1, a2, b1, b2))
-
-        for half in range(2):
-            a1, a2, b1, b2 = picked[half]
+            a2 = look_up(first, a, list2, half, "a2")
+            a1 = look_up(first, a, list1, half, "a1")
             pieces = [slice(k * PIECE, (k + 1) * PIECE) for k in range(2)]
             kept = [sb.tile([P, PIECE], F32, name="kept%d_%d" % (half, k)) for k in range(2)]
             swapped = [sb.tile([P, PIECE], F32, name="swapped%d_%d" % (half, k)) for k in range(2)]
@@ -150,6 +152,10 @@ def tile_attend_exchanged_lean_throughtwo_heads_kernel(
         for half in range(2):
             y4 = look_up(False, f2, list4, half, "y4_%d" % half)
             y3 = look_up(True, f2, list3, half, "y3_%d" % half)
-            y = sb.tile([P, HALF], F32, name="y%d" % half)
-            nc.vector.tensor_tensor(y[:], y3[:], y4[:], ALU.max)
-            nc.sync.dma_start(out=out[:, half * HALF : (half + 1) * HALF], in_=y[:])
+            bounds = (0, HALF) if half == 0 else (0, PIECE, HALF)
+            for k in range(len(bounds) - 1):
+                lo, hi = bounds[k], bounds[k + 1]
+                y = sb.tile([P, hi - lo], F32, name="y%d_%d" % (half, k))
+                nc.vector.tensor_tensor(y[:], y3[:, lo:hi], y4[:, lo:hi], ALU.max)
+                queue = nc.scalar if (half, k) == (1, 0) else nc.sync
+                queue.dma_start(out=out[:, half * HALF + lo : half * HALF + hi], in_=y[:])

@@ -124,14 +124,14 @@ def tile_attend_exchanged_lean_throughtwo_heads_kernel(
                 nc.scalar.activation(got[:], window, COPY)
             return got
 
-        a = scores(0, "a", (3,))
-        b = scores(1, "b", ())
+        a = scores(0, "a", ())
+        b = scores(1, "b", (3,))
 
         for half in range(2):
             first = half == 0
             b1 = look_up(False, b, list1, half, "b1_%d" % half)
             b2 = look_up(first, b, list2, half, "b2_%d" % half)
-            a2 = look_up(first, a, list2, half, "a2")
+            a2 = look_up(first, a, list2, half, "a2_%d" % half)
             a1 = look_up(first, a, list1, half, "a1")
             pieces = [slice(k * PIECE, (k + 1) * PIECE) for k in range(2)]
             kept = [sb.tile([P, PIECE], F32, name="kept%d_%d" % (half, k)) for k in range(2)]

from contextlib import ExitStack

import concourse.mybir as mybir

D, T, I, Q = 512, 1024, 512, 128
FLOPS = 2 * 2 * D * T * Q

F32 = mybir.dt.float32
BF16 = mybir.dt.bfloat16
I32 = mybir.dt.int32
U32 = mybir.dt.uint32
U16 = mybir.dt.uint16
U8 = mybir.dt.uint8
FP8X4 = mybir.dt.float8_e4m3fn_x4
ALU = mybir.AluOpType
COPY = mybir.ActivationFunctionType.Copy

P = 128
PACK = 4
CHUNK = 256
HALF = I // 2
PIECE = HALF // 2
STRIPE = 16
KEY_LOADS = ((0, 3 * CHUNK), (3 * CHUNK, T))


def tile_attend_exchanged_lean_throughtwo_heads_kernel(
    tc, query, query2, keys_words, keys_scales, lam, old, offs, offs2, offs3, offs4, out
):
    nc = tc.nc
    with ExitStack() as ctx:
        sb = ctx.enter_context(tc.tile_pool(name="sb", bufs=1))
        ps = ctx.enter_context(tc.psum_pool(name="ps", bufs=1))

        def entries(lst, start, count):
            return lst[:, start // STRIPE : (start + count) // STRIPE]

        key_scales = sb.tile([P, CHUNK], U8, align_bytes=64, name="key_scales")
        nc.gpsimd.memset(key_scales[:].bitcast(I32), 0)
        scale_rows = keys_scales[0].bitcast(I32)

        words_hbm = keys_words[0].rearrange("p n t -> p (n t)").bitcast(I32)
        raw = []
        key_words = []
        for h, src in enumerate((query, query2)):
            r = sb.tile([P, PACK, Q], F32, name="raw%d" % h)
            nc.sync.dma_start(out=r[:], in_=src.rearrange("(p j) q -> p j q", j=PACK))
            raw.append(r)
            if h == 0:
                for quad in range(4):
                    nc.sync.dma_start(
                        out=key_scales[32 * quad : 32 * quad + 16, :].bitcast(I32),
                        in_=scale_rows[4 * quad : 4 * quad + 4, :].rearrange("r (c n) -> c r n", c=4),
                    )
            lo, hi = KEY_LOADS[h]
            kw = sb.tile([P, hi - lo], I32, align_bytes=64, name="key_words%d" % h)
            nc.sync.dma_start(out=kw[:], in_=words_hbm[:, lo:hi])
            key_words.append(kw)

        list1 = sb.tile([P, I // STRIPE], U16, name="list1")
        nc.sync.dma_start(list1[:], offs)
        list2 = sb.tile([P, I // STRIPE], U16, name="list2")
        nc.sync.dma_start(list2[:], offs2)
        lam_col = sb.tile([P, 1], F32, name="lam_col")
        nc.sync.dma_start(out=lam_col[:], in_=lam)
        old_sb = sb.tile([P, T], F32, name="old_sb")
        nc.sync.dma_start(out=old_sb[:], in_=old)
        list3 = sb.tile([P, I // STRIPE], U16, name="list3")
        nc.sync.dma_start(list3[:], offs3)
        list4 = sb.tile([P, I // STRIPE], U16, name="list4")
        nc.sync.dma_start(list4[:], offs4)

        f1 = sb.tile([P, T], F32, name="f1")
        nc.vector.memset(f1[:], 0.0)
        lam_wide = sb.tile([P, PIECE], F32, name="lam_wide")
        nc.gpsimd.tensor_scalar(lam_wide[:], lam_col[:].to_broadcast([P, PIECE]), 1.0, 0.0, ALU.mult, ALU.add)

        codes = []
        for h in range(2):
            grouped = sb.tile([P, Q, PACK], BF16, align_bytes=64, name="grouped%d" % h)
            shares = ((nc.vector.tensor_copy, 0, Q // 2), (nc.scalar.copy, Q // 2, Q)) if h == 0 else ((nc.vector.tensor_copy, 0, Q),)
            for copy, lo, hi in shares:
                copy(
                    out=grouped[:, lo:hi, :].rearrange("p (c i) t -> p c t i", i=4),
                    in_=raw[h][:, :, lo:hi].rearrange("p t (c i) -> p c t i", i=4),
                )
            qc = sb.tile([P, Q], U32, align_bytes=64, name="q_codes%d" % h)
            qs = sb.tile([P, Q], U8, align_bytes=64, name="q_scales%d" % h)
            nc.vector.quantize_mx(
                out=qc[:].bitcast(FP8X4), scales=qs[:], in_=grouped[:].rearrange("p q t -> p (q t)")
            )
            codes.append((qc, qs))

        def scores(h, name, on_vector):
            table = sb.tile([P, T], F32, name=name)
            qc, qs = codes[h]
            for c in range(T // CHUNK):
                bank = ps.tile([P, CHUNK], F32, name="bank_%s%d" % (name, c))
                part = c * CHUNK // KEY_LOADS[1][0]
                kw = key_words[part]
                k0 = c * CHUNK - KEY_LOADS[part][0]
                nc.tensor.matmul_mx(
                    out=bank[:],
                    lhsT=qc[:].bitcast(FP8X4),
                    lhsT_scale=qs[:],
                    rhs=kw[:, k0 : k0 + CHUNK].bitcast(FP8X4),
                    rhs_scale=key_scales[4 * c : P, :],
                    start=True,
                    stop=True,
                )
                cols = table[:, c * CHUNK : (c + 1) * CHUNK]
                if c in on_vector:
                    nc.vector.tensor_copy(out=cols, in_=bank[:])
                else:
                    nc.scalar.copy(out=cols, in_=bank[:])
            return table

        def look_up(on_vector, table, lst, half, name):
            got = sb.tile([P, HALF], F32, name=name)
            window = table[:].indirect(entries(lst, half * HALF, HALF))
            if on_vector:
                nc.vector.tensor_copy(got[:], window)
            else:
                nc.scalar.activation(got[:], window, COPY)
            return got

        a = scores(0, "a", ())
        b = scores(1, "b", (3,))

        for half in range(2):
            first = half == 0
            b1 = look_up(False, b, list1, half, "b1_%d" % half)
            b2 = look_up(first, b, list2, half, "b2_%d" % half)
            a2 = look_up(first, a, list2, half, "a2_%d" % half)
            a1 = look_up(first, a, list1, half, "a1")
            pieces = [slice(k * PIECE, (k + 1) * PIECE) for k in range(2)]
            kept = [sb.tile([P, PIECE], F32, name="kept%d_%d" % (half, k)) for k in range(2)]
            swapped = [sb.tile([P, PIECE], F32, name="swapped%d_%d" % (half, k)) for k in range(2)]
            diff = [sb.tile([P, PIECE], F32, name="diff%d_%d" % (half, k)) for k in range(2)]
            for k in range(2):
                nc.vector.tensor_tensor(swapped[k][:], a2[:, pieces[k]], b1[:, pieces[k]], ALU.max)
                nc.vector.tensor_tensor(kept[k][:], a1[:, pieces[k]], b2[:, pieces[k]], ALU.max)
            for k in range(2):
                nc.vector.tensor_tensor(diff[k][:], kept[k][:], swapped[k][:], ALU.subtract)
            for k in range(2):
                places = f1[:].indirect(entries(list1, half * HALF + k * PIECE, PIECE))
                nc.vector.tensor_tensor(places, diff[k][:], lam_wide[:], ALU.mult)

        f2 = sb.tile([P, T], F32, name="f2")
        nc.vector.tensor_tensor(f2[:], f1[:], old_sb[:], ALU.add)

        for half in range(2):
            y4 = look_up(False, f2, list4, half, "y4_%d" % half)
            y3 = look_up(True, f2, list3, half, "y3_%d" % half)
            bounds = (0, HALF) if half == 0 else (0, PIECE, HALF)
            for k in range(len(bounds) - 1):
                lo, hi = bounds[k], bounds[k + 1]
                y = sb.tile([P, hi - lo], F32, name="y%d_%d" % (half, k))
                nc.vector.tensor_tensor(y[:], y3[:, lo:hi], y4[:, lo:hi], ALU.max)
                queue = nc.scalar if (half, k) == (1, 0) else nc.sync
                queue.dma_start(out=out[:, half * HALF + lo : half * HALF + hi], in_=y[:])
